import numpy as np, ml_dtypes
CORES = [6,15,38,47]
N = 4
BF = ml_dtypes.bfloat16
E, D, R, NB, M, PH, P = 4096, 256, 512, 1, 9, 3, 4
S = NB + 2 - PH % 2
def link(rng, a, b):
    k = np.arange(E); k[:D] += D; k[a] = b
    s = np.setdiff1d(np.arange(D, E), a); t = np.setdiff1d(np.concatenate([np.arange(D), np.arange(2 * D, E)]), b)
    k[s] = rng.permutation(t)
    return k
def near(rng, n):
    return link(rng, 2 * D + rng.permutation(R)[:n], rng.permutation(D)[:n])
def ways(rng, late, fresh):
    pool = 2 * D + R + rng.permutation(E - 2 * D - R); at = [0]; o = 2 * D + rng.permutation(R); tab = [([], []), ([], [])]
    def join(a, b, t):
        tab[t & 1][0].append(a); tab[t & 1][1].append(b)
    def go(a, t, n):
        for i in range(t, t + n):
            b = pool[at[0]:at[0] + len(a)]; at[0] += len(a)
            join(a, b, i); a = b
        return a
    if late:
        join(go(o[:D], 0, PH), rng.permutation(D), PH); go(o[D:], 0, PH + 1)
    else:
        w = go(o[:D], 0, PH - 1); join(w, rng.permutation(D), PH - 1)
        u = go(o[D:], 0, 2 * PH); s = go(D + np.arange(D), PH, PH)
        m = np.concatenate([u, s]); to = m
        if PH % 2 == 0:
            m = np.concatenate([m, w]); to = np.concatenate([to, o[:D]])
        if fresh: go(m, 2 * PH, 1)
        else: join(m, rng.permutation(to), 2 * PH)
    return [link(rng, np.concatenate(a), np.concatenate(b)) for a, b in tab]
def both(rng, one):
    p = [[one(r, g) for g in range(8)] for r in range(N)]
    return [np.array([[p[r][g][i] for g in range(8)] for r in range(N)]) for i in range(2)]
def some(rng):
    return both(rng, lambda r, g: (near(rng, int(rng.integers(D // 8, D // 2))), near(rng, int(rng.integers(0, D // 2)))))
def values(rng):
    e = rng.choice(np.array([0.5, 1.0, 2.0]), (N, 8, 1, E))
    x = np.minimum(np.floor(16 * rng.random((N, 8, 16, E)) ** e), 15).astype(np.int64)
    q = np.minimum(np.floor(16 * rng.random((N, 8, 16, R)) * rng.random((N, 8, 1, R))), 15).astype(np.int64)
    return x, q
def pack(k, x, q):
    return {"k0": k[0].astype(np.int32), "k1": k[1].astype(np.int32), "x": np.ascontiguousarray(x.reshape(N, 128, E)).astype(np.float32).astype(BF),
            "q": np.ascontiguousarray(q.reshape(N, 128, R)).astype(np.float32).astype(BF)}
def setup_inputs(rng):
    x, q = values(rng)
    return pack(some(rng), x, q)
def setup_inputs_full(rng):
    x, q = values(rng)
    def one(r, g):
        if r < S: return ways(rng, False, r > NB)
        if g == 6: return ways(rng, True, False)
        if g == 7: return [link(rng, D + rng.permutation(D), rng.permutation(D)) for i in range(2)]
        n = (D, D, D - 1, D, 1, D // 2)[g]
        return near(rng, n), near(rng, D // 4)
    q[:, :5] = 0
    x[:S] = rng.integers(13, 16, (S, 8, 16, E)); q[:S] = rng.integers(0, 14, (S, 8, 16, R))
    x[S:, 6] = rng.integers(13, 16, (N - S, 16, E)); q[S:, 6] = rng.integers(0, 14, (N - S, 16, R))
    return pack(both(rng, one), x, q)
def setup_inputs_ties(rng):
    hi = rng.integers(4, 16, (N, 8, 1, 1)); cnt = rng.integers(M - 1, M + 2, (N, 8, 1, E)); off = 2 * rng.integers(0, 2, (N, 8, 1, E))
    top = np.argsort(rng.random((N, 8, E, 16)), axis=-1).transpose(0, 1, 3, 2) < cnt
    x = hi - 1 + top - off; q = np.broadcast_to(hi - 2 * rng.integers(0, 2, (N, 8, 1, R)), (N, 8, 16, R))
    return pack(some(rng), x, q)
def setup_inputs_chain(rng):
    def one(r, g):
        h = D // 2
        return [link(rng, np.concatenate([2 * D + rng.permutation(R)[:h], D + rng.permutation(D)[:D - h]]), rng.permutation(D)) for i in range(2)]
    x = rng.integers(10, 16, (N, 8, 16, E)); q = rng.integers(0, 9, (N, 8, 16, R))
    return pack(both(rng, one), x, q)
def setup_inputs_ends(rng):
    x, q = values(rng)
    def one(r, g):
        a = np.arange(2 * D, E)
        if g == 2: return [link(rng, a, a) for i in range(2)]
        if g == 3:
            k = near(rng, D // 2); return k, k
        u = np.array([2 * D, 2 * D + R - 1, 2 * D + 1]); w = np.array([0, D - 1, E - 1])
        return link(rng, u, w), link(rng, u, w[::-1])
    x[:, 0] = 0; q[:, 0] = 0; x[:, 1] = 15; q[:, 1] = 15; x[:, 6] = 0; q[:, 6] = rng.integers(0, 3, (N, 1, R))
    q[..., 0] = 0; q[..., 1] = 0; q[..., R - 1] = 0
    return pack(both(rng, one), x, q)
def setup_inputs_spread(rng):
    x = np.minimum(np.floor(np.exp2(4 * rng.random((N, 8, 1, E))) * rng.random((N, 8, 16, E))), 15).astype(np.int64)
    q = np.minimum(np.floor(np.exp2(4 * rng.random((N, 8, 1, R))) * rng.random((N, 8, 16, R))), 15).astype(np.int64)
    c = np.array([0, 1, D // 2, D])
    return pack(both(rng, lambda r, g: (near(rng, int(rng.choice(c))), near(rng, int(rng.choice(c))))), x, q)
def check_inputs(d):
    bad = []
    for k in ("k0", "k1"):
        v = np.asarray(d[k]).astype(np.int64)
        if np.any(np.sort(v, axis=-1) != np.arange(E)): bad.append(k + " is no permutation")
        if np.any(v[..., :D] != D + np.arange(D)): bad.append("doors of " + k)
    for k in ("x", "q"):
        v = np.asarray(d[k]).astype(np.float64)
        if not np.all((v >= 0) & (v <= 15) & (v == np.rint(v))): bad.append("range of " + k)
    return bad
def reference(k0, k1, x, q):
    k = np.stack([k0, k1]).astype(np.int64)
    X = x.astype(np.float32).astype(np.int64).reshape(N, 8, 16, E)
    Q = np.concatenate([q.astype(np.float32).astype(np.int64).reshape(N, 8, 16, R), np.zeros((N, 8, 16, D), np.int64)], axis=3)
    first = np.concatenate([2 * D + np.arange(R), D + np.arange(D)])
    v = np.tile(first, (N, 8, 1)); b = v.copy()
    act = np.zeros((N, 8, R + D), bool); act[:, :, :R] = True
    mark = np.zeros((N, 8, E), bool); mark[:, :, 2 * D:2 * D + R] = True
    turn = np.zeros((N, 8, E), np.int64); wait = np.zeros((N, 8, R + D), bool)
    def enough(hi, lo, axis):
        return np.add.reduce((hi >= lo).astype(np.int64), axis=axis) >= M
    def retreat(m):
        Q[:] = Q - m[:, :, None, :].astype(np.int64)
        n, g, w = np.nonzero(m & (b != v))
        p = b[n, g, w]; o = v[n, g, w]; h = turn[n, g, p]; back = k[h, n, g, p]
        xo = X[n, g, :, o]; xp = X[n, g, :, p]
        k[h, n, g, p] = np.where(enough(xo, xp, 1), o, p)
        X[n, g, :, p] = np.maximum(xp, xo - 1)
        b[n, g, w] = back; v[n, g, w] = p
    for t in range(PH * P):
        f = t & 1
        go = act & (v >= D)
        c = np.take_along_axis(k[f], v, 2)
        ok = go & ~np.take_along_axis(mark, c, 2) & enough(np.take_along_axis(X, c[:, :, None, :], 3), Q, 2)
        n, g, w = np.nonzero(ok); o = v[n, g, w]; to = c[n, g, w]
        k[f, n, g, o] = b[n, g, w]; turn[n, g, o] = f; mark[n, g, to] = True
        Q[n, g, :, w] = np.maximum(Q[n, g, :, w], X[n, g, :, to]) - 2
        b[n, g, w] = o; v[n, g, w] = to
        retreat(go & ~ok)
        if t % PH == PH - 1:
            on = act & (v < D); stay = on & wait; new = on & ~wait
            n, g, w = np.nonzero(new); j = v[n, g, w]; to = (n + 1 + j // (D // NB)) % N
            Q[to, g, :, R + j] = Q[n, g, :, w]; act[to, g, R + j] = True; mark[to, g, D + j] = True
            n, g, w = np.nonzero(stay); j = v[n, g, w]; to = (n + 1 + j // (D // NB)) % N
            X[n, g, :, j] = X[to, g, :, D + j]
            retreat(stay)
            wait = new
    return {"yk0": k[0].astype(np.float32), "yk1": k[1].astype(np.float32), "yx": X.reshape(N, 128, E).astype(np.float32).astype(BF)}

from concourse.mybir import AluOpType, ActivationFunctionType

A = AluOpType
F = ActivationFunctionType
E, NW, NS = 4096, 768, 12
DVB, LB = 4112, 4928
WIN = LB + (NS + 1) * NW
BIG = 16384.0
CUT = 6
K0H, K1H, IDH, K0L, K1L, IDL, DOOR, ONE, ND, PS, PH, PL, PAR, SF0, SF1, FR = range(16)

ZS = ["zcnt", "zc0", "zc1", "zid", "zext", "zp"]
MS = ["mi", "mni", "md", "mn0", "mn1", "mp", "msg", "mini", "mgv", "m64", "mn64", "mh"]

SCRATCH = {
    "xin": ("sbuf", [128, E], "bfloat16"),
    "qin": ("sbuf", [128, 512], "bfloat16"),
    "w": ("sbuf", [128, E], "float32"),
    "wb": ("sbuf", [128, E], "bfloat16"),
    "xw": ("sbuf", [128, WIN], "bfloat16"),
    "kw": ("sbuf", [128, WIN], "bfloat16"),
    "pl": ("sbuf", [128, 2 * NW], "float32"),
    "hf": ("sbuf", [128, 13 * 48], "float32"),
    "hi32": ("sbuf", [128, 13 * 48], "int32"),
    "lo": ("sbuf", [128, 48], "float32"),
    "ki": ("sbuf", [128, 512], "int32"),
    "kh": ("sbuf", [128, 512], "int32"),
    "kl": ("sbuf", [128, 512], "int32"),
    "kf32": ("sbuf", [128, 768], "float32"),
    "dk": ("sbuf", [128, 512], "float32"),
    "nt": ("sbuf", [128, 11 * 256], "bfloat16"),
    "zz": ("sbuf", [128, 144 * len(ZS)], "bfloat16"),
    "mm": ("sbuf", [128, 8 * len(MS), 16], "bfloat16"),
    "pint": ("sbuf", [128, 16], "int32"),
    "pand": ("sbuf", [128, 16], "int32"),
    "pf": ("sbuf", [128, 16], "float32"),
    "r15": ("sbuf", [128, 16], "float32"),
    "sc": ("sbuf", [128, 16], "float32"),
    "tf": ("sbuf", [128, 13 * 48], "float32"),
    "et": ("sbuf", [128, 256], "float32"),
    "nq": ("sbuf", [128, 16 + NW], "bfloat16"),
    "tq": ("sbuf", [128, NW], "bfloat16"),
    "cmp": ("sbuf", [128, NW + 256], "bfloat16"),
    "xm": ("sbuf", [128, NW], "bfloat16"),
    "sg": ("sbuf", [128, NW], "bfloat16"),
    "gv": ("sbuf", [128, 4 * 256], "bfloat16"),
    "sw": ("sbuf", [128, 3 * 256], "bfloat16"),
    "lq": ("sbuf", [128, 3 * 256], "bfloat16"),
    "ld": ("sbuf", [128, 3 * 256], "bfloat16"),
    "sm": ("sbuf", [128, 16 * 48], "float32"),
    "oc": ("sbuf", [128, 48], "uint16"),
    "ok2": ("sbuf", [128, 48], "uint16"),
    "om": ("sbuf", [128, 48], "uint16"),
    "oq": ("sbuf", [128, 48], "uint16"),
    "oid": ("sbuf", [128, 48], "uint16"),
    "osw": ("sbuf", [128, 48], "uint16"),
    "ptf": ("sbuf", [128, 256], "float32"),
    "opk": ("sbuf", [128, 256], "uint16"),
    "opx": ("sbuf", [128, 64], "uint16"),
    "kfin": ("sbuf", [128, E], "bfloat16"),
    "xfin": ("sbuf", [128, E], "bfloat16"),
    "nf": ("sbuf", [128, 7 * 256], "bfloat16"),
    "m1": ("sbuf", [128, 512], "float32"),
    "m2": ("sbuf", [128, 512], "float32"),
    "yy": ("sbuf", [128, 512], "float32"),
    "b0": ("psum", [128, 512], "float32"),
    "b1": ("psum", [128, 512], "float32"),
    "b27": ("psum", [128, 1024], "float32"),
    "b34": ("psum", [128, 1024], "float32"),
    "b56": ("psum", [128, 1024], "float32"),
}
NDMA = 72
SEMAPHORES = ["cv", "cs", "ct", "cg"] + ["d%d" % i for i in range(NDMA)] + \
    ["aq0", "aq1", "aq2", "ad0", "ad1", "ad2", "sq0", "sq1", "sq2", "sd0", "sd1", "sd2"]


def rank_program(g, core, T, topo):
    rank = T.rank_of(core)
    if rank is None:
        return
    n_ranks = len(T.cores)
    nxt, prv = T.cores[(rank + 1) % n_ranks], T.cores[(rank - 1) % n_ranks]

    Q = {"v": g.vector, "s": g.scalar, "t": g.tensor, "g": g, "y": g.sync}
    cnt = {"v": 0, "s": 0, "t": 0, "g": 0}
    seen = {q: {} for q in Q}
    lastw, readers, total = {}, {}, {}
    ndma = [0]

    def wait(q, tok):
        if seen[q].get(tok[0], 0) < tok[1]:
            Q[q].wait_ge(T.sem[tok[0]], tok[1])
            seen[q][tok[0]] = tok[1]

    def order(q, R, W):
        need = {}
        for k in R:
            for tk in lastw.get(k, []):
                need[tk[0]] = max(need.get(tk[0], 0), tk[1])
        for k in W:
            for tk in lastw.get(k, []) + readers.get(k, []):
                need[tk[0]] = max(need.get(tk[0], 0), tk[1])
        for s in need:
            wait(q, (s, need[s]))

    def note(tok, R, W):
        total[tok[0]] = max(total.get(tok[0], 0), tok[1])
        for k in R:
            readers.setdefault(k, []).append(tok)
        for k in W:
            lastw[k] = [tok]
            readers[k] = []

    def op(q, fn, R, W):
        order(q, R, W)
        ins = fn()
        cnt[q] += 1
        ins.then_inc(T.sem["c" + q], 1)
        note(("c" + q, cnt[q]), R, W)

    def dma(q, out, in_, R, W, after=()):
        order(q, R, list(W) + list(after))
        s = "d%d" % ndma[0]
        ndma[0] += 1
        Q[q].dma_start(out, in_).then_inc(T.sem[s], 16)
        note((s, 16), R, W)

    def mms(items, R, W):
        def run():
            ins = None
            for (o, l, r, st, sp) in items:
                ins = g.tensor.matmul(o, l, r, st, sp)
            return ins
        op("t", run, R, W)

    def send(dst, out, in_, rsem, lsem, R):
        order("g", R, [])
        rid, pid, _ = topo.addr(dst)
        g.remote_dma(out, in_, T.sem[rsem], T.sem[lsem], pid, rid, topo.mask(core, dst))
        note((lsem, len(topo.engines(core, dst))), R, [])

    def arrival(src, rsem, key):
        note((rsem, len(topo.engines(src, core))), [], [key])

    V, S = g.vector, g.scalar

    def ts(out, in0, s1, s2, o0, o1, R, W):
        if s2 is None:
            op("v", lambda: V.tensor_scalar(out, in0, s1, None, o0), R, W)
        else:
            op("v", lambda: V.tensor_scalar(out, in0, s1, s2, o0, o1), R, W)

    def tt(out, a, b, o, R, W):
        op("v", lambda: V.tensor_tensor(out, a, b, o), R, W)

    def cp(out, a, R, W):
        op("v", lambda: V.tensor_copy(out, a), R, W)

    def ms(ap, c, W):
        op("v", lambda: V.memset(ap, c), [], W)

    def act(out, in_, f, R, W, bias=0.0, scale=1.0):
        op("s", lambda: S.activation(out, in_, f, bias, scale), R, W)

    def iota(out, pat, base, cm, W, flt=True):
        if flt:
            op("g", lambda: g.iota(out, pat, base, cm, allow_small_or_imprecise_dtypes=True), [], W)
        else:
            op("g", lambda: g.iota(out, pat, base, cm), [], W)

    def zview(name):
        o = 144 * ZS.index(name)
        return T.zz[:, o + 15:o + 143:16]

    def zl(name, i):
        o = 144 * ZS.index(name)
        return T.zz[:, o + 15 - i:o + 143 - i]

    def mat(name):
        o = 8 * MS.index(name)
        return T.mm[:, o:o + 8, :]

    def zset(name, row, val):
        v = zview(name)
        op("g", lambda: g.affine_select(v, v, [[-16, 8]], A.not_equal, float(val), -row, 1), [], [name])

    def mset(name, row, c0, c1, val):
        o = 8 * MS.index(name)
        v = T.mm[:, o:o + 8, c0:c1]
        op("g", lambda: g.affine_select(v, v, [[-16, 8], [0, c1 - c0]], A.not_equal, float(val), -row, 1), [], [name])

    def diag(name, val):
        v = mat(name)
        op("g", lambda: g.affine_select(v, v, [[-16, 8], [-1, 16]], A.not_equal, float(val), 0, 1), [], [name])

    def band(v, name, width):
        p1 = [[-16, 8]] + ([[0, width]] if width else [])
        p2 = [[16, 8]] + ([[0, width]] if width else [])
        op("g", lambda: g.affine_select(v, v, p1, A.is_ge, 0.0, 0, 1), [], [name])
        op("g", lambda: g.affine_select(v, v, p2, A.is_ge, 0.0, 15, -1), [], [name])

    def to_list(z, out, buf, c0, ncol, R, W, first=True, final=True):
        mms([(out, zl(z, i), buf[:, c0 + i:c0 + ncol:16], first and i == 0, final and i == 15) for i in range(16)],
            [z] + R, W)

    def wide(out, lo, terms, R, W, first=True, final=True):
        items = []
        for (a, b) in ((lo, 512), (512, NW)):
            for j, (m, buf, c0) in enumerate(terms):
                items.append((out[:, a:b], mat(m), buf[:, c0 + a:c0 + b], first and j == 0,
                              final and j == len(terms) - 1))
        mms(items, [m for (m, _, _) in terms] + R, W)

    def sm(j, lo=0):
        return T.sm[:, 48 * j + lo:48 * j + 48]

    def slot(s):
        return LB + NW * s

    def ntc(j):
        return T.nt[:, 256 * j:256 * j + 256]

    KS = ["ks%d" % r for r in range(16)] + ["kgap"]

    dma("y", T.ki[:, 0:256], T.k0[:], [], ["ki0"])
    dma("s", T.ki[:, 256:512], T.k1[:], [], ["ki1"])
    dma("y", T.xin[:, 0:2048], T.x[:, 0:2048], [], ["xa"])
    dma("s", T.xin[:, 2048:E], T.x[:, 2048:E], [], ["xb"])
    dma("s", T.qin[:], T.q[:], [], ["qin"])
    iota(T.pint[:, 0:1], [[0, 1]], 0, 1, ["pint"], False)
    iota(ntc(IDH), [[1, 4], [0, 64]], 0, 0, ["nt2"])
    iota(ntc(IDL), [[0, 4], [1, 64]], 0, 0, ["nt5"])
    ms(ntc(8), 1.0, ["nt8"])
    ms(ntc(9), 0.0, ["nt9"])
    ms(ntc(10), -1.0, ["nt10"])
    C3, K3 = T.nt[:, 2048:2816], ["nt8", "nt9", "nt10"]
    act(T.w[:, 256:1024], C3, F.Silu, K3, ["wr"], bias=64.0, scale=0.0)
    for b in (0, 1):
        act(T.pl[:, NW * b:NW * b + NW], C3, F.Identity, K3, ["pl%d" % b], bias=64.0, scale=0.0)
    act(T.kw[:, E:E + NW], C3, F.Identity, K3, ["kgap"], scale=0.0)
    act(T.kw[:, E + NW:LB], T.nt[:, 2048:2048 + LB - E - NW], F.Identity, K3, ["kgap"], scale=0.0)
    ts(T.pand[:, 0:1], T.pint[:, 0:1], 15, None, A.bitwise_and, None, ["pint"], ["pand"])
    ms(T.zz[:], 0.0, ZS)
    cp(T.pf[:, 0:1], T.pand[:, 0:1], ["pand"], ["pf"])
    ms(zview("zcnt"), -BIG, ["zcnt"])
    ts(T.pf[:, 2:3], T.pf[:, 0:1], 4.0, None, A.mult, None, ["pf"], ["pf2"])
    ms(T.mm[:], 0.0, MS)
    ts(ntc(IDH), ntc(IDH), T.pf[:, 2:3], None, A.add, None, ["pf2"], ["nt2"])
    osg = 8 * MS.index("msg")
    ms(T.mm[:, osg:osg + 8, SF0:SF1 + 1], -8.0, ["msg"])
    ts(ntc(6), ntc(IDH), 4.0, None, A.is_lt, None, ["nt2"], ["nt6"])
    ts(T.pf[:, 1:2], T.pf[:, 0:1], 48.0, -31.5, A.mult, A.add, ["pf"], ["pf1"])
    ts(ntc(7), ntc(6), -1.0, -2.0, A.mult, A.add, ["nt6"], ["nt7"])
    for r, j in ((ONE, 8), (PS, 9), (PH, 9), (PL, 9), (PAR, 9), (SF0, 9), (SF1, 9), (FR, 10), (IDL, 5), (IDH, 2),
                 (DOOR, 6), (ND, 7)):
        dma("y", T.kw[r:128:16, 0:E], ntc(j), ["nt%d" % j], ["ks%d" % r])
    KI = ["ki0", "ki1"]
    ts(T.kh[:], T.ki[:], 6, None, A.arith_shift_right, None, KI, ["kh"])
    ts(T.kl[:], T.ki[:], 63, None, A.bitwise_and, None, KI, ["kl"])
    cp(T.nt[:, 0:512], T.kh[:], ["kh"], ["nth"])
    for r in (K0H, K1H):
        dma("y", T.kw[r:128:16, 0:E], ntc(r), ["nth"], ["ks%d" % r])
    cp(T.nt[:, 768:1280], T.kl[:], ["kl"], ["ntl"])
    for r in (K0L, K1L):
        dma("y", T.kw[r:128:16, 0:E], ntc(r), ["ntl"], ["ks%d" % r])
    iota(T.hf[:], [[NW, 13], [1, 48]], LB - 64, 0, ["hf"])
    zset("zc0", K0H, 64.0)
    band(zview("zcnt"), "zcnt", 0)
    zset("zc0", K0L, 1.0)
    mset("mini", ONE, ND, ND + 1, -1.0)
    zset("zc0", ONE, -4096.0)
    mset("mp", IDH, PH, PH + 1, 1.0)
    mset("mini", ONE, PS, PS + 1, 512.0)
    mset("mp", IDL, PL, PL + 1, 1.0)
    iota(T.sc[:, 0:12], [[1, 12]], -1, 0, ["sc"])
    mset("mp", PS, SF0, SF1 + 1, -1.0)
    zset("zid", IDH, 64.0)
    mset("mp", PAR, SF0, SF0 + 1, -256.0)
    zset("zid", IDL, 1.0)
    mset("mp", PAR, SF1, SF1 + 1, 256.0)
    iota(T.tf[:], [[NW, 13], [16, 48]], LB, 0, ["tf"])
    mset("md", ND, 0, 16, -1.0)
    zset("zc1", K1H, 64.0)
    zset("zext", PS, 768.0)
    mset("md", DOOR, 0, 16, -1.0)
    zset("zc1", K1L, 1.0)
    zset("zext", FR, -768.0)
    mset("mn0", ONE, ND, ND + 1, -1.0)
    zset("zc1", ONE, -4096.0)
    mset("mn0", ND, PS, PAR + 1, -128.0)
    zset("zext", DOOR, BIG)
    mset("mn0", DOOR, PS, PAR + 1, -128.0)
    mset("mn0", ONE, PS, PAR + 1, -256.0)
    mset("mn0", FR, PS, PS + 1, -1.0)
    mset("mn0", ND, SF0, SF1 + 1, 256.0)
    mset("mn0", DOOR, SF0, SF1 + 1, -256.0)
    mset("mn0", ONE, SF0, SF0 + 1, 272.0)
    mset("mn0", ONE, SF1, SF1 + 1, 16.0)
    diag("mi", 1.0)
    diag("mni", -1.0)
    band(T.mm[:, osg:osg + 8, SF0:SF1 + 1], "msg", 2)
    act(T.xw[:, 3072:E], T.xin[:, 3072:E], F.Identity, ["xb"], ["x0c"], scale=-1.0)
    act(T.w[:, 0:256], T.xin[:, 0:256], F.Identity, ["xa"], ["wa"], scale=-1.0)
    act(T.w[:, 1024:2048], T.xin[:, 1024:2048], F.Identity, ["xa"], ["wb_"], scale=-1.0)
    act(T.w[:, 2048:E], T.xin[:, 2048:E], F.Identity, ["xb"], ["wc"], scale=-1.0)
    ts(T.hi32[:], T.hf[:], T.pf[:, 1:2], 1.0 / 64, A.add, A.mult, ["hf", "pf1"], ["hi32"])
    ts(T.lo[:], T.hf[:, 0:48], T.pf[:, 1:2], 95.5, A.add, A.add, ["hf", "pf1"], ["lo"])
    cp(T.hf[:], T.hi32[:], ["hi32"], ["hf"])
    ts(T.nq[:, 272:16 + NW], T.qin[:], -1.0, None, A.mult, None, ["qin"], ["nqw"])
    ts(sm(9), T.hf[:, 0:48], -64.0, None, A.mult, None, ["hf"], ["s9"])
    ms(T.xw[:, E:LB], 64.0, ["xpad", "dv"])
    tt(T.lo[:], T.lo[:], sm(9), A.add, ["s9"], ["lo"])
    ts(T.xw[:, 0:2048], T.xin[:, 0:2048], -1.0, None, A.mult, None, ["xa"], ["x0a"])
    ts(T.xw[:, 2048:3072], T.xin[:, 2048:3072], -1.0, None, A.mult, None, ["xb"], ["x0b"])
    X0 = ["x0a", "x0b", "x0c", "xpad"]

    def payload(t):
        b = t & 1
        dma("y", T.pl[0:128:16, NW * b:NW * b + NW], T.hf[:, 48 * t + 48:48 * t + 96], ["hf", "pl%d" % b], ["plh%d" % b])

    for b in (0, 1):
        dma("y", T.pl[1:128:16, NW * b:NW * b + NW], T.lo[:], ["lo", "pl%d" % b], ["pll%d" % b])
        payload(b)
    dma("y", T.w[0:128:16, 256:1024], T.hf[:, 0:48], ["hf"], ["wr0"], ["wr"])
    dma("y", T.w[1:128:16, 256:1024], T.lo[:], ["lo"], ["wr1"], ["wr"])
    to_list("zc0", T.b1[:, 80:112], T.kw, 512, 512, KS[:16], ["b1"])
    wide(T.b56, 0, [("mp", T.kw, 256), ("mini", T.kw, 256)], KS[:16], ["b56"])
    ts(sm(6, 16), T.b1[:, 80:112], 256.0 - E, float(E), A.is_ge, A.mult, [], ["b1", "s6"])
    ts(sm(7, 16), T.b1[:, 80:112], 1024.0 - E, None, A.is_lt, None, [], ["b1", "s7"])
    ts(sm(8, 16), T.b1[:, 80:112], float(E), None, A.add, None, [], ["b1", "s8"])
    tt(sm(6, 16), sm(6, 16), sm(7, 16), A.mult, ["s7"], ["s6"])
    tt(sm(7, 16), sm(6, 16), sm(8, 16), A.max, ["s6", "s8"], ["s7"])
    cp(T.oc[:, 16:48], sm(7, 16), ["s7"], ["oc"])
    dma("y", T.xw[:, slot(0):slot(1)], T.xw[:, 256:1024], ["x0a"], ["xl0"])
    for s in (1, 2, 3):
        dma("y", T.xw[:, slot(s):slot(s) + 256], T.xw[:, 256:512], ["x0a"], ["xg%d" % s])
    dma("y", T.gv[:, 0:256], T.xw[:, 256:512], ["x0a"], ["gv0"])

    def first_step():
        ts(T.r15[:, 0:1], T.pf[:, 0:1], float(FR), None, A.is_equal, None, ["pf"], ["r15"])
        tt(T.kw[:, slot(0):slot(1)], T.kw[:, 256:1024], T.b56[:, 0:NW], A.max, KS[:16], ["k0", "b56"])
        ts(sm(0, 16), T.tf[:, 16:48], T.pf[:, 0:1], None, A.add, None, ["tf", "pf"], ["ir"])
        ts(T.sc[:, 0:12], T.sc[:, 0:12], T.r15[:, 0:1], 1.0, A.mult, A.add, ["r15", "sc"], ["sc"])
        for s in (1, 2, 3):
            dma("y", T.kw[:, slot(s):slot(s) + 256], T.kw[:, slot(0):slot(0) + 256], ["k0"], ["kg%d" % s])
        dma("y", T.kw[PAR:128:16, slot(1):slot(1) + 256], T.nt[0:8, 2048:2304], ["nt8"], ["kg1"])

    def idle_work(t):
        if t == 0:
            cp(mat("mn1"), mat("mn0"), ["mn0"], ["mn1"])
            mset("mn1", ONE, PAR, PAR + 1, -255.0)
        if t == 1:
            zset("zp", 0, 64.0)
            zset("zp", 1, 1.0)
            ms(T.nq[:, 0:272], -128.0, ["nqg"])
            mset("mgv", ONE, 0, 16, 65.0)
            mset("mgv", PS, 0, 16, -0.125)
            iota(T.et[:], [[16, 256]], 0, 0, ["et"])
            iota(T.kf32[:, 512:768], [[1, 256]], 0, 0, ["idf"])
            ts(T.pf[:, 3:4], T.pf[:, 0:1], 256.0, None, A.mult, None, ["pf"], ["pf3"])
        if t == 3:
            diag("m64", 64.0)
            diag("mn64", -64.0)
            diag("mh", 0.5)
            cp(T.kf32[:, 0:512], T.ki[:], KI, ["kf32"])
            ts(T.kf32[:, 512:768], T.kf32[:, 512:768], T.pf[:, 3:4], None, A.add, None, ["pf3"], ["idf"])
            ts(T.et[:], T.et[:], T.pf[:, 0:1], None, A.add, None, ["pf"], ["et"])
            for f in (0, 1):
                tt(T.dk[:, 256 * f:256 * f + 256], T.kf32[:, 512:768], T.kf32[:, 256 * f:256 * f + 256],
                   A.subtract, ["kf32", "idf"], ["dk%d" % f])

    WK = ["wa", "wb_", "wc", "wr", "wr0", "wr1"]

    def kwin(s):
        return KS + ["k%d" % j for j in range(s + 1)] + ["k%dg" % j for j in range(s + 1)] + \
            ["kg%d" % j for j in range(1, min(s, 3) + 1)]

    def xwin(s):
        return X0 + ["dv"] + ["xl%d" % j for j in range(s + 1)] + ["xg%d" % j for j in range(1, min(s, 3) + 1)]

    def patch(t):
        lo = 256 if t < 3 else 0
        v = T.kw[:, slot(t + 1) + lo:slot(t + 2)]
        tt(v, v, T.b56[:, lo:NW], A.max, [], ["k%d" % (t + 1), "k%dg" % (t + 1), "b56"])

    gvk = [0]
    banks = [(T.b0, 0, "b0"), (T.b1, 0, "b1"), (T.b34, 0, "b34"), (T.b34, 512, "b34")]

    def narrow(qs, e):
        for q in qs:
            if e == "v":
                cp(T.wb[:, 1024 * q:1024 * q + 1024], T.w[:, 1024 * q:1024 * q + 1024], WK, ["wb%d" % q])
            else:
                act(T.wb[:, 1024 * q:1024 * q + 1024], T.w[:, 1024 * q:1024 * q + 1024], F.Identity, WK, ["wb%d" % q])

    def places(qs):
        for q in qs:
            bk, bo, bn = banks[q]
            to_list("zp", bk[:, bo:bo + 64], T.wb, 1024 * q, 1024, ["wb%d" % q], [bn])

    for t in range(NS):
        lo = 256 if t < 3 else 0
        ml = lo // 16
        last = t == NS - 1
        release = t in (5, 8, 11)
        sending = t in (2, 5, 8)
        new = "k%d" % (t + 1)
        NQ = ["nqw", "nqg"] if t > 2 else ["nqw"]
        if t in (3, 6, 9):
            p = t // 3 - 1
            lqp = T.lq[:, 256 * p:256 * p + 256]
            tt(T.cmp[:, 256:NW], T.w[:].indirect(T.oc[:, 16:48]), T.nq[:, 272:16 + NW], A.is_le, WK + ["oc", "nqw"],
               ["cmpw"])
            to_list("zcnt", T.b0[:, 16:48], T.cmp, 256, 512, ["cmpw"], ["b0"])
            if t > 3:
                tt(T.cmp[:, 0:256], T.w[:].indirect(T.oc[:, 0:16]), T.nq[:, 16:272], A.is_le, WK + ["oc", "nqg"],
                   ["cmpg"])
                to_list("zcnt", T.b0[:, 0:16], T.cmp, 0, 256, ["cmpg"], ["b0"], True, False)
            else:
                patch(t - 1)
                idle_work(t)
            arrival(prv, "aq%d" % p, "lq%d" % p)
            tt(T.cmp[:, NW:NW + 256], T.w[:].indirect(T.oc[:, 0:16]), lqp, A.is_le, WK + ["oc", "lq%d" % p], ["cmpn"])
            to_list("zcnt", T.b0[:, 0:16], T.cmp, NW, 256, ["cmpn"], ["b0"], t == 3, True)
            if t > 3:
                patch(t - 1)
        else:
            win, wk = (T.w[:], WK) if t else (T.xw[:, 0:DVB], X0)
            tt(T.cmp[:, lo:NW], win.indirect(T.oc[:, ml:48]), T.nq[:, 16 + lo:16 + NW], A.is_le, wk + ["oc"] + NQ,
               ["cmpw", "cmpg"])
            to_list("zcnt", T.b0[:, ml:48], T.cmp, lo, NW - lo, ["cmpw", "cmpg"], ["b0"])
            if t:
                patch(t - 1)
            else:
                first_step()
        if t + 1 < NS and t:
            payload(t + 1)
        ts(sm(1, ml), T.b0[:, ml:48], 9 * BIG + 4096.0, 4096.0, A.add, A.max, [], ["b0", "u"])
        tt(sm(2, ml), sm(1, ml), T.b1[:, 64 + ml:112], A.add, ["u"], ["b1", "cu"])
        tt(sm(3, ml), sm(2, ml), sm(0, ml), A.min, ["cu", "ir"], ["ik"])
        cp(T.ok2[:, ml:48], sm(3, ml), ["ik"], ["ok2"])
        for (a, b, key) in (((0, 256, new + "g"), (256, NW, new)) if release else ((lo, NW, new),)):
            act(T.kw[:, slot(t + 1) + a:slot(t + 1) + b], T.kw[:, 0:slot(t + 1)].indirect(T.ok2[:, a // 16:b // 16]),
                F.Identity, kwin(t) + ["ok2", "sc"], [key], scale=T.sc[:, t:t + 1])
        newk = [new, new + "g"]
        if not last:
            ts(T.oq[:, ml:48], sm(2, ml), 4096.0, None, A.min, None, ["cu"], ["oq"])
        if t:
            tm = sm(4, ml) if release else T.tf[:, 48 * t + ml:48 * t + 48]
            tt(sm(5, ml), sm(1, ml), tm, A.min, ["u", "tm", "tf"], ["im"])
            cp(T.om[:, ml:48], sm(5, ml), ["im"], ["om"])
        if t in (3, 6, 9):
            tt(T.nq[:, 16:272], T.nq[:, 16:272], lqp, A.max, ["lq%d" % p], ["nqg"])

        def gv_sum():
            mms([(T.b0[:, 256:512], mat("mi"), T.xw[:, slot(t):slot(t) + 256], True, False),
                 (T.b0[:, 256:512], mat("mgv"), T.kw[:, slot(t + 1):slot(t + 1) + 256], False, True)],
                ["mi", "mgv", new + "g" if release else new, "xl%d" % t, "xg3"], ["b0"])

        def do_gv(tg):
            src = gvk[0]
            dst = src
            if tg in (7, 10):
                dst = src + 1
                gvk[0] = dst
            tt(T.gv[:, 256 * dst:256 * dst + 256], T.gv[:, 256 * src:256 * src + 256], T.b0[:, 256:512], A.min,
               ["gv%d" % src], ["gv%d" % dst, "b0"])

        def do_xm(a, b, q):
            src = T.xw[:, 0:slot(t + 1)].indirect(T.om[:, a // 16:b // 16])
            if q == "s":
                act(T.xm[:, a:b], src, F.Identity, xwin(t) + ["om"], ["xm" + q], bias=1.0)
            else:
                ts(T.xm[:, a:b], src, 1.0, None, A.add, None, xwin(t) + ["om"], ["xm" + q])

        def send_q():
            p = t // 3
            swp = T.sw[:, 256 * p:256 * p + 256]
            to_list("zp", T.b0[:, 128:144], T.wb, 0, 256, ["wb0"], ["b0"])
            ts(T.osw[:, 0:16], T.b0[:, 128:144], 16.0 - slot(t + 1), 0.0, A.add, A.max, [], ["b0", "osw"])
            cp(swp, T.nq[:].indirect(T.osw[:, 0:16]), ["osw", "nqw", "nqg"], ["sw%d" % p])
            send(nxt, T.lq[:, 256 * p:256 * p + 256], swp, "aq%d" % p, "sq%d" % p, ["sw%d" % p])

        def do_xl():
            o = T.xw[:, slot(t + 1) + lo:slot(t + 2)]
            src = T.xw[:, 0:slot(t + 1)].indirect(T.ok2[:, ml:48])
            if t:
                tt(o, src, T.xm[:, lo:NW], A.min, xwin(t) + ["ok2", "xms", "xmv"], ["xl%d" % (t + 1)])
            else:
                cp(o, src, xwin(t) + ["ok2"], ["xl1"])

        if release:
            p = t // 3 - 1
            do_gv(t - 1)
            gv_sum()
            do_gv(t)
            send(prv, T.ld[:, 256 * p:256 * p + 256], T.gv[:, 256 * gvk[0]:256 * gvk[0] + 256], "ad%d" % p, "sd%d" % p,
                 ["gv%d" % gvk[0]])
        if not last:
            tt(T.tq[:, lo:NW], T.xw[:, 0:DVB].indirect(T.oq[:, ml:48]), T.nq[:, 16 + lo:16 + NW], A.min,
               X0 + ["oq"] + NQ, ["tq"])
        lo2 = 256 if t < 2 else 0
        m2 = lo2 // 16
        cut = lo + (NW - lo) * CUT // 8 // 32 * 32
        if t and not release:
            do_xm(cut, NW, "v")
        to_list("zid", T.b1[:, ml:48], T.kw, slot(t + 1) + lo, NW - lo, newk, ["b1"])
        if t and not release:
            do_xm(lo, cut, "s")
        cp(T.oid[:, ml:48], T.b1[:, ml:48], [], ["b1", "oid"])
        op("s", lambda: S.activation(T.w[:].indirect(T.oid[:, ml:48]), T.pl[:, NW * (t & 1) + lo:NW * (t & 1) + NW],
                                     F.Silu),
           ["oid", "pl%d" % (t & 1), "plh%d" % (t & 1), "pll%d" % (t & 1)], WK)
        if not last:
            wide(T.b34, lo, [("md", T.kw, slot(t + 1))], newk, ["b34"])
            if t and not release:
                wide(T.b27, lo, [("mni", T.xm, 0)], ["xms", "xmv"], ["b2", "b7"], True, False)
            to_list("zc%d" % ((t + 1) & 1), T.b1[:, 64 + m2:112], T.kw, slot(t + 1) + lo2, NW - lo2,
                    newk + ["kg3"] * (t == 2), ["b1"])
            to_list("zext", T.b0[:, 64 + m2:112], T.kw, slot(t + 1) + lo2, NW - lo2, newk + ["kg3"] * (t == 2), ["b0"])
        if t in (4, 7, 10):
            gv_sum()
        pterms = [("mn%d" % (t & 1), T.kw, slot(t + 1)), ("mp", T.kw, slot(t))]
        pkeys = newk + ["k%d" % t, "k%dg" % t] + ["kg3"] * (t == 3)
        if last:
            wide(T.b34, lo, pterms, pkeys, ["b34"])
        if t == 0 or release:
            wide(T.b56, lo, pterms, pkeys, ["b56"], True, t == 0)
        if not release and not sending:
            do_xl()
        if sending:
            act(T.wb[:, 0:256], T.w[:, 0:256], F.Identity, WK, ["wb0"])
        if not last:
            tt(T.nq[:, 16 + lo:16 + NW], T.tq[:, lo:NW], T.b34[:, lo:NW], A.add, ["tq"], NQ + ["b34"])
        if t == 2:
            do_xl()
            send_q()
        if t == 0:
            ts(T.tf[:], T.tf[:], T.pf[:, 0:1], None, A.add, None, ["pf"], ["tf"])
        if last:
            tt(T.tq[:], T.kw[:, slot(NS):slot(NS + 1)], T.b34[:, 0:NW], A.max, newk, ["tq", "b34"])
            old = ["k%d" % j for j in range(NS)] + ["kg1", "kg2", "kg3", "k6g", "k9g"]
            for (a, b) in ((PH, ND), (PL, ONE), (PAR, DOOR)):
                dma("y", T.kw[b:128:16, slot(0):slot(NS - 1)], T.kw[a:128:16, slot(1):slot(NS)], [], ["kn%d" % b], old)
                dma("y", T.kw[b:128:16, slot(NS - 1):slot(NS)], T.tq[a:128:16, :], ["tq"], ["ko%d" % b], old)
            narrow((0, 1), "s")
        if release:
            p = t // 3 - 1
            arrival(nxt, "ad%d" % p, "ld%d" % p)
            cp(T.xw[:, DVB + 256 * p:DVB + 256 * p + 256], T.ld[:, 256 * p:256 * p + 256], ["ld%d" % p], ["dv"])
            do_xm(0, NW, "v")
            if sending:
                send_q()
            do_xl()
        if t:
            if release:
                wide(T.b27, lo, [("mni", T.xm, 0)], ["xms", "xmv"], ["b2", "b7"], True, False)
            wide(T.b27, lo, [("mi", T.xw, slot(t + 1))], ["xl%d" % (t + 1)], ["b2", "b7"], False, True)
            if not release:
                wide(T.b56, lo, pterms, pkeys, ["b56"], True, False)
            if last:
                places((0, 1))
                narrow((2, 3), "v")
            act(T.sg[:, lo:NW], T.b27[:, lo:NW], F.Sign, [], ["sg", "b2", "b7"], bias=1.5)
            wide(T.b56, lo, [("msg", T.sg, 0)], ["sg"], ["b56"], False, True)
        if not last:
            ts(T.oc[:, m2:48], T.b1[:, 64 + m2:112], 4096.0, None, A.add, None, [], ["b1", "oc"])
            ext = T.b0[:, 64 + m2:112]
            if t + 1 in (5, 8, 11):
                p = (t + 1) // 3 - 1
                ts(sm(8), ext, BIG, None, A.is_ge, None, [], ["b0", "s8"])
                ts(sm(9), ext, BIG + 768.0 * (t - 1), -BIG, A.is_lt, A.mult, [], ["b0", "s9"])
                tt(sm(10), sm(8), sm(9), A.mult, ["s8", "s9"], ["s10"])
                tt(sm(8), sm(10), ext, A.add, ["s10"], ["b0", "s8"])
                tt(sm(9), sm(10), T.b1[:, 0:48], A.add, ["s10"], ["b1", "s9"])
                ts(sm(11), sm(8), 768.0 * (t + 1), None, A.min, None, ["s8"], ["s11"])
                ts(sm(10), sm(9), BIG + DVB + 256.0 * p, None, A.add, None, ["s9"], ["s10"])
                tt(sm(0), sm(11), T.tf[:, 0:48], A.add, ["s11", "tf"], ["ir"])
                tt(sm(4), sm(10), T.tf[:, 48 * (t + 1):48 * (t + 2)], A.min, ["s10", "tf"], ["tm"])
            else:
                ts(sm(11, m2), ext, 768.0 * (t + 1), None, A.min, None, [], ["b0", "s11"])
                tt(sm(0, m2), sm(11, m2), T.tf[:, m2:48], A.add, ["s11", "tf"], ["ir"])
        if t < 3:
            idle_work(t)

    act(T.b27[:, 0:512], T.dk[:], F.Identity, ["dk0", "dk1"], ["b2"])
    act(T.b27[:, 512:1024], T.kf32[:, 0:512], F.Identity, ["kf32"], ["b7"])
    places((2, 3))
    patch(NS - 1)
    for q in range(4):
        bk, bo, bn = banks[q]
        tt(T.ptf[:, 64 * q:64 * q + 64], bk[:, bo:bo + 64], T.et[:, 64 * q:64 * q + 64], A.max, ["et"],
           [bn, "ptf%d" % q])
    cp(T.opk[:], T.ptf[:], ["ptf0", "ptf1", "ptf2", "ptf3"], ["opk"])
    KW = kwin(NS) + ["kn%d" % b for b in (ND, ONE, DOOR)] + ["ko%d" % b for b in (ND, ONE, DOOR)]
    cp(T.kfin[:, 0:2048], T.kw[:].indirect(T.opk[:, 0:128]), KW + ["opk"], ["kf0"])
    act(T.kfin[:, 2048:E], T.kw[:].indirect(T.opk[:, 128:256]), F.Identity, KW + ["opk"], ["kf1"])
    for j, r in enumerate((ND, ONE, DOOR, PH, PL, SF0, SF1)):
        dma("y", T.nf[:, 256 * j:256 * j + 256], T.kfin[r:128:16, :], ["kf0", "kf1"], ["nf%d" % j])
    d = T.ptf[:, 0:16]
    ts(sm(1, 32), d, float(slot(6)), 256.0, A.is_ge, A.mult, ["ptf0"], ["u"])
    ts(sm(2, 32), d, float(slot(9)), 256.0, A.is_ge, A.mult, ["ptf0"], ["cu"])
    ts(sm(3, 32), d, float(LB), None, A.is_lt, None, ["ptf0"], ["ik"])
    ts(sm(5, 32), d, float(slot(12)), None, A.is_ge, None, ["ptf0"], ["im"])
    tt(sm(6, 32), sm(1, 32), sm(2, 32), A.add, ["u", "cu"], ["s6"])
    tt(sm(7, 32), sm(3, 32), sm(5, 32), A.add, ["ik", "im"], ["s7"])
    cp(T.opx[:, 16:64], T.ptf[:, 16:64], ["ptf0"], ["opxb"])
    tt(sm(8, 32), sm(6, 32), T.et[:, 0:16], A.add, ["s6", "et"], ["s8"])
    ts(sm(9, 32), sm(7, 32), BIG, float(DVB), A.mult, A.add, ["s7"], ["s9"])
    tt(sm(10, 32), sm(8, 32), sm(9, 32), A.add, ["s8", "s9"], ["s10"])
    tt(sm(11, 32), sm(10, 32), d, A.min, ["s10", "ptf0"], ["s11"])
    cp(T.opx[:, 0:16], sm(11, 32), ["s11"], ["opxa"])

    def xq(q, n=1024):
        off = T.opx[:, 0:64] if q == 0 else T.opk[:, q // 16:(q + n) // 16]
        R = xwin(NS) + (["opxa", "opxb"] if q == 0 else ["opk"])
        o = T.xfin[:, q:q + n]
        if q == 0:
            ts(o, T.xw[:].indirect(off), -1.0, None, A.mult, None, R, ["xf%d" % q])
        else:
            act(o, T.xw[:].indirect(off), F.Identity, R, ["xf%d" % q], scale=-1.0)
        dma("y" if q == 0 else "s", T.yx[:, q:q + n], o, ["xf%d" % q], ["yx%d" % q])

    xq(0)
    xq(1024)
    xq(2048)
    xq(3072, 512)
    xq(3584, 512)

    def nfc(j):
        return T.nf[:, 256 * j:256 * j + 256]

    mms([(T.b0[:, 0:256], mat("mn64"), ntc(IDH), True, False), (T.b0[:, 0:256], mat("mni"), ntc(IDL), False, False),
         (T.b0[:, 0:256], mat("m64"), nfc(0), False, False), (T.b0[:, 0:256], mat("mi"), nfc(1), False, False),
         (T.b0[:, 0:256], mat("mh"), nfc(2), False, True)],
        ["mn64", "mni", "m64", "mi", "mh", "nth", "ntl", "nt2", "nt5", "nf0", "nf1", "nf2"], ["b0"])
    items = []
    for f in (0, 1):
        o = T.b1[:, 256 * f:256 * f + 256]
        items += [(o, mat("mn64"), ntc(K0H + f), True, False), (o, mat("mni"), ntc(K0L + f), False, False),
                  (o, mat("m64"), nfc(3), False, False), (o, mat("mi"), nfc(4), False, True)]
    mms(items, ["nf3", "nf4"], ["b1"])
    ts(T.m2[:], T.nf[:, 1280:1792], 0.0, None, A.is_gt, None, ["nf5", "nf6"], ["m2"])
    ts(T.m1[:, 0:256], T.b0[:, 0:256], 0.0, None, A.is_equal, None, [], ["b0", "m1a"])
    tt(T.m2[:], T.m2[:], T.b27[:, 0:512], A.mult, [], ["m2", "b2"])
    ts(T.m1[:, 256:512], T.b0[:, 0:256], 0.5, None, A.is_equal, None, [], ["b0", "m1b"])
    tt(T.b27[:, 512:1024], T.m2[:], T.b27[:, 512:1024], A.add, ["m2"], ["b7"])
    tt(T.m1[:], T.m1[:], T.b1[:], A.mult, [], ["m1a", "m1b", "b1"])
    for f in (0, 1):
        tt(T.yy[:, 256 * f:256 * f + 256], T.m1[:, 256 * f:256 * f + 256], T.b27[:, 512 + 256 * f:768 + 256 * f], A.add,
           ["m1a", "m1b"], ["yy%d" % f, "b7"])
        dma("y", (T.yk0 if f == 0 else T.yk1)[:], T.yy[:, 256 * f:256 * f + 256], ["yy%d" % f], ["yk%d" % f])
    for s in total:
        wait("y", (s, total[s]))
